import numpy as np, ml_dtypes
CORES = [66,74,82,90,194,202,210,218]
N = 8
import mx_ref
BF = ml_dtypes.bfloat16
def gentries(a):
    return np.ascontiguousarray(a.reshape(8, 16, -1).transpose(0, 2, 1)).reshape(8, -1)
def gtable(e):
    e = np.asarray(e); return np.ascontiguousarray(e.reshape(8, -1, 16).transpose(0, 2, 1)).reshape(128, -1).astype(np.int32)
def gcols(t, e):
    v = np.concatenate([t.reshape(8, 16, -1, 4), np.zeros((8, 16, 1, 4), BF)], axis=2)
    return np.ascontiguousarray(np.stack([v[g][:, e[g]] for g in range(8)])).reshape(128, -1)
def tile(rs):
    return np.stack(rs, axis=2).reshape(128, -1).astype(BF)
def cut(t, i, w=512):
    return t[:, w * i:w * i + w]
def pick(q, e):
    c = np.concatenate([q[0].reshape(128, -1, 4), np.zeros((128, 1, 4), np.uint8)], axis=1); s = np.concatenate([q[1], np.ones((16, 1), np.uint8)], axis=1)
    return (np.ascontiguousarray(c[:, e].reshape(128, -1)), np.ascontiguousarray(s[:, e]))
def join(*qs):
    return (np.concatenate([q[0] for q in qs], axis=1), np.concatenate([q[1] for q in qs], axis=1))
def put(q, e, v):
    c, s = q[0].reshape(128, -1, 4).copy(), q[1].copy(); c[:, e] = v[0].reshape(128, -1, 4); s[:, e] = v[1]
    return (c.reshape(128, -1), s)
def pk(c, s):
    return (np.ascontiguousarray(c), mx_ref.live(s))
def emit(q):
    return q[0], q[1]
def packed(v, rng):
    q = [mx_ref.quantize(np.ascontiguousarray(v[r])) for r in range(N)]
    return np.stack([a for a, b in q]), np.stack([mx_ref.plane(b, rng) for a, b in q])
def values_of_codes():
    e, c = np.zeros((128, 128, 4), np.float32), np.zeros((128, 2, 4), np.uint8)
    e[np.arange(128), np.arange(128), 0] = 1
    c[:127, :, 0] = np.arange(256).reshape(2, 128).T[:127]
    return mx_ref.matmul(mx_ref.quantize(e.reshape(128, 512).astype(BF)), (c.reshape(128, 8), np.full((16, 2), 127, np.uint8))).T.reshape(-1).astype(np.float64)
CODE_VALUE, SCALE_VALUE = values_of_codes(), 2.0 ** (np.arange(256) - 127.0)
def decode(q):
    return (CODE_VALUE[q[0]].reshape(16, 8, -1, 4) * SCALE_VALUE[q[1]][:, None, :, None] + 0.0).reshape(128, -1).astype(np.float32)
def f(rng, *shape):
    return mx_ref.flush((rng.standard_normal(shape, dtype=np.float32) * np.exp2(rng.integers(-2, 3, shape[:-1] + (1,)))).astype(BF))
def wide(rng, *shape, cols=0):
    v = rng.standard_normal(shape, dtype=np.float32) * np.exp2(rng.integers(-12, 13, shape)).astype(np.float32)
    if cols: v *= np.repeat(np.exp2(rng.integers(-cols, cols + 1, shape[:-2] + (1, shape[-1] // 4))) * (rng.random(shape[:-2] + (1, shape[-1] // 4)) > 0.0625), 4, axis=-1).astype(np.float32)
    return mx_ref.flush(v.astype(BF))
C, P, E, T, R = 352, 32, 4, 128, 3
STEP = [1, 2, 4]
OPPOSITE = np.array([E * (P - 1 - q) + i for q in range(P) for i in range(E)])
def sow(n, s):
    o, m = np.zeros((8, C), int), np.zeros((8, P), int)
    for g in range(8):
        end = np.cumsum(n[g])
        mark = np.where(n[g] > 0, s[g][np.maximum(end - 1, 0)] + np.float32(0.0), np.float32(-np.inf))
        chosen = 4 * np.arange(P // 4) + np.argmax(mark.reshape(-1, 4), axis=1)
        pit = np.repeat(np.arange(P), n[g])
        k = np.arange(C) - (end - n[g])[pit]
        moved = np.isin(pit, chosen)
        to = np.where(moved, (pit + 1 + k) % P, pit)
        o[g] = np.lexsort((k, moved, to))
        m[g] = np.bincount(to, minlength=P)
    return o, m
def ends(n):
    i = np.arange(E)
    return np.where(i < n[:, :, None], np.cumsum(n, axis=1)[:, :, None] - 1 - i, -1).reshape(8, T)
def gput(t, e, h):
    a, b = t.reshape(8, 16, -1, 4).copy(), h.reshape(8, 16, -1, 4)
    for g in range(8):
        j = np.flatnonzero(e[g] >= 0)
        a[g][:, e[g][j]] = b[g][:, j]
    return a.reshape(128, -1)
def big(v):
    v = v.astype(np.float32)
    v[np.abs(v) < np.float32(2.0 ** -16)] = 0
    return v.astype(BF)
def numbers_of(rng):
    return {"x": big(f(rng, N, 128, 4 * C)), "u": np.array(f(rng, N, 128, 512)), "v": np.array(f(rng, N, 128, 512))}
def weights(rng, still=[]):
    w = big(f(rng, N, 128, 2048)).reshape(N, 8, 16, 4, 8, 16, 4)
    for i in still:
        w[:, :, i] = 0
        w[:, :, :, :, :, i] = 0
    c, p = packed(w.reshape(N, 128, 2048), rng)
    return {"wc": c, "ws": p}
def sizes(rng):
    n = np.zeros((N, 8, P), int)
    for r in range(N):
        for g in range(8):
            m = rng.integers(0, P, P)
            n[r, g] = np.bincount(m[rng.integers(0, P, C)], minlength=P)
    return n
def stored(n):
    return np.stack([gtable(a) for a in n])
def signs(rng):
    return np.stack([rng.permutation(8) % 2 * 2.0 - 1.0 for r in range(N)])
def setup_inputs(rng):
    return {**numbers_of(rng), **weights(rng), "sz": stored(sizes(rng))}
def setup_inputs_ties(rng):
    d = numbers_of(rng)
    e = rng.permutation(N)
    x = d["x"].reshape(N, 8, 16, C, 4)
    for r in range(N):
        k = np.zeros(C, int) if r == e[0] else rng.permutation(C) % 3
        a = x[r][:, :8, :3].copy()
        a[:, :, 2] = 0
        x[r][:, :8] = a[:, :, k]
    x[e[1]] = 0
    u = d["u"].reshape(N, 8, 16, 8, 16, 4)
    k = u.copy()
    u[:, :, :, :, 0] = 0
    for g in range(8): u[:, g, :8, g, 0] = k[:, g, :8, g, 0]
    return {"x": x.reshape(N, 128, 4 * C), "u": u.reshape(N, 128, 512), "v": d["v"], **weights(rng, range(8)), "sz": stored(sizes(rng))}
def setup_inputs_near(rng):
    d = numbers_of(rng)
    n = sizes(rng)
    x = d["x"].astype(np.float32).reshape(N, 8, 16, C, 4)
    x[:, :, 0] = 0
    x[:, :, 8:] = 0
    u = d["u"].reshape(N, 128, 128, 4)
    u[:, :, ::16] = 0
    o, c = rng.permutation(N) % 4, signs(rng)
    for r in range(N):
        if o[r] == 3:
            x[r, :, 9:] = rng.integers(8, 16, (8, 7, C, 4)) * 2.0 ** -30
            x[r, :, 9] = 0
            stays = rng.permutation(8) < 4
            for g in range(8):
                h, m = int(rng.integers(1, 5)), 4 * int(rng.integers(0, P // 4))
                if stays[g]: h = 1
                n[r, g] = 0
                n[r, g, m] = h
                n[r, g, m + 1 if stays[g] else m + 3] = C - h
                s = rng.integers(8, 10, C)
                s[h - 1], s[C - 1] = (9, 8) if stays[g] else (8, 9)
                x[r, g, 8, :, 0] = s * 2.0 ** -30
        else:
            size = 1.0 if o[r] < 2 else 2.0 ** -4
            s = (np.arange(C) + rng.integers(0, C, (8, 1))) % C // 8
            z = ((s[:, :, None] >> np.arange(8)) & 1) * np.exp2(np.arange(8) - 23.0) * size
            if o[r] < 2: x[r, :, 0, :, 0] = c[r][:, None]
            x[r, :, 8] = z[:, :, :4]
            x[r, :, 9] = z[:, :, 4:]
            x[r, :, 10:] = rng.integers(4, 8, (8, 6, C, 4)) * 2.0 ** -20 * size
        k = 1.0 if o[r] == 0 else 2.0 ** -30
        for h in range(0, 128, 16):
            u[r, h, h, 0] = k
            u[r, h + 8:h + 10, h] = k
    return {"x": x.reshape(N, 128, 4 * C).astype(BF), "u": u.reshape(N, 128, 512), "v": d["v"], **weights(rng, [0, 8, 9, 10, 11, 12, 13, 14, 15]), "sz": stored(n)}
def setup_inputs_huge(rng):
    d = numbers_of(rng)
    n = sizes(rng)
    c = np.stack([rng.permutation(C) % 2 * 2.0 - 1.0 for r in range(N)])
    r, z = np.arange(N), int(rng.integers(N))
    one = np.isin(r, [z] + [z ^ s for s in STEP])
    c[one] = ((r ^ (r >> 1) ^ (r >> 2)) % 2 * 2.0 - 1.0)[one][:, None]
    k = rng.random((N, 128, C, 4))
    x = 2.0 ** 30 * np.where(one[:, None, None, None], 0.75 + 0.125 * k, 0.08 + 0.01 * k) * c[:, None, :, None]
    x[z, :, C - 1] = 2.0 ** 30 * c[z, C - 1]
    for m in n[z]:
        m[P - 1] = np.sum(m[P - 4:])
        m[P - 4:P - 1] = 0
        m[np.argmax(m)] -= 1
        m[P - 1] += 1
    u = d["u"].reshape(N, 128, 128, 4)
    a = 2.0 ** 30 * (1 - 0.1 * rng.random((N, 128, 8, 4))) * signs(rng)[:, None, :, None]
    a[z] = 2.0 ** 30 * np.sign(a[z])
    u[:, :, ::16] = a.astype(np.float32).astype(BF)
    w = np.zeros((N, 128, 4, 128, 4), np.float32)
    i = np.arange(128)
    for b in range(4): w[:, i, b, i, b] = -1
    wc, ws = packed(w.reshape(N, 128, 2048).astype(BF), rng)
    return {"x": x.astype(np.float32).reshape(N, 128, 4 * C).astype(BF), "u": u.reshape(N, 128, 512), "v": d["v"], "wc": wc, "ws": ws, "sz": stored(n)}
def setup_inputs_pits(rng):
    d = setup_inputs(rng)
    n = np.zeros((N, 8, P), int)
    for r in range(N):
        k = rng.permutation(8)
        for g in range(8):
            m = n[r, g]
            q = 4 * rng.permutation(P // 4) + rng.integers(0, 4, P // 4)
            if k[g] == 0: m[q[0]] = C
            if k[g] == 1: m[P - 1] = C
            if k[g] == 2:
                m[q[:3]] = P - 1, P, P + 1
                m += np.bincount(4 * (q[3:] // 4)[rng.integers(0, P // 4 - 3, C - 3 * P)] + rng.integers(0, 4, C - 3 * P), minlength=P)
            if k[g] == 3 and r % 2 == 0: m += np.bincount(q[np.arange(C) % (P // 4)], minlength=P)
            if k[g] == 3 and r % 2 == 1:
                i = int(rng.integers(0, P // 4))
                m[3::4] = 4 * ((i - 1 - np.arange(P // 4)) % (P // 4)) + 1
                m[4 * (q[0] // 4) + 3] += C - np.sum(m)
            if k[g] == 4: m += np.bincount(np.arange(C) % P, minlength=P)
            if k[g] == 5:
                m[:] = rng.permutation(np.arange(P) % (E + 2))
                m[q[0]] += C - np.sum(m)
            if k[g] == 6: m[q[:2]] = C - 1, 1
            if k[g] == 7: m[q[:2]] = 2 * P, C - 2 * P
    d["sz"] = stored(n)
    return d
def setup_inputs_spread(rng):
    d = setup_inputs(rng)
    d["x"] = big(wide(rng, N, 128, 4 * C, cols=6))
    return d
def check_inputs(d):
    b = []
    for k in ("x", "u", "v"):
        a = np.abs(d[k].astype(np.float32))
        if not (np.isfinite(a).all() and ((a == 0) | (a >= 2.0 ** -30) & (a <= 2.0 ** 30)).all()): b.append("a value of " + k)
    if ((d["wc"] & 0x7F) == 0x7F).any(): b.append("a code of wc that is no number")
    z = np.zeros((128, 4, 4), np.float32)
    z[:, 1] = 2.0 ** -30
    z[:, 2] = 2.0 ** 30
    c, s = emit(mx_ref.quantize(z.reshape(128, 16).astype(BF)))
    for r in range(N):
        p = mx_ref.live(d["ws"][r])
        if not ((p == s[0, 0]) | (p >= s[0, 1]) & (p <= s[0, 2])).all(): b.append("a scale of ws")
        n = gentries(d["sz"][r]).astype(np.int64)
        if (n < 0).any(): b.append("a size of sz below 0")
        if (np.sum(n, axis=1) != C).any(): b.append("the sum of a group's sizes")
    return b
def reference(x, u, v, wc, ws, sz):
    qu = [mx_ref.quantize(u[r]) for r in range(N)]
    lay = [pk(wc[r], ws[r]) for r in range(N)]
    now = [x[r] for r in range(N)]
    n = [gentries(sz[r]) for r in range(N)]
    for t in range(R):
        own, sent = [], []
        for r in range(N):
            o, n[r] = sow(n[r], mx_ref.matmul(qu[r], mx_ref.quantize(now[r]))[::16])
            now[r] = gcols(now[r], o)
            own.append(gcols(now[r], ends(n[r])))
            sent.append(mx_ref.quantize(own[r]))
        came = decode(join(*sent))
        for r in range(N):
            c = cut(came, r ^ STEP[t], 4 * T).reshape(128, T, 4)[:, OPPOSITE].reshape(128, 4 * T)
            q = mx_ref.quantize((own[r].astype(np.float32) + c).astype(BF))
            h = tile([mx_ref.matmul(pick(lay[r], np.arange(128 * b, 128 * b + 128)), q) * np.float32(0.015625) + own[r][:, b::4].astype(np.float32) for b in range(4)])
            now[r] = gput(now[r], ends(n[r]), h)
    y, oz = np.zeros((N, 128, C), np.float32), np.zeros((N, 8, P), np.float32)
    oc, osc = np.zeros((N, 128, 4 * C), np.uint8), np.zeros((N, 16, C), np.uint8)
    for r in range(N):
        q = mx_ref.quantize(now[r])
        y[r] = mx_ref.matmul(mx_ref.quantize(v[r]), q)
        oz[r] = n[r]
        oc[r], osc[r] = emit(q)
    return {"y": y, "oz": oz, "oc": oc, "osc": osc}

from concourse.mybir import dt, AluOpType, AxisListType, ActivationFunctionType

C, NP, R = 352, 32, 3
PAD, HB, PL = 32, 384, 512
XW = 4 * (PAD + C)
O0, GW = 392, 504
K = 34
LV = 98
Z = 131072.0
BIG = 1048576.0
CUT = (0, 224, C)
AV = 1
XV = ((0, 0), (1, 0))
F32, BF, I32, U16, U8, X4 = "float32", "bfloat16", "int32", "uint16", "uint8", "float8_e4m3fn_x4"
CY = 1.04
CASES = ((100.0, 1.5, 3.5, 4200.0), (60.0, 1.2, 2.0, 4500.0), (170.0, 1.9, 5.5, 3500.0), (100.0, 1.5, 3.5, 5500.0),
         (100.0, 1.5, 3.5, 3000.0))
TRIES = 120

SCRATCH = {"ps": ("psum", [128, 4096], F32)}
POOL = {}


def _sb(names, n, d):
    for s in names.split():
        SCRATCH[s] = ("sbuf", [128, n], d)


def _pool(buf, d, *parts):
    a = 16
    for names, n in parts:
        for s in names.split():
            POOL[s] = (buf, a, n)
            a += n
    SCRATCH[buf] = ("sbuf", [128, a], d)


_sb("X0 X1 X2 X3", XW, BF)
_sb("Wn0 Wn1 Wn2 Et", 2048, BF)
_sb("A0 A1 A2 B0 B1 B2 A64 ut vt onb", 512, BF)
_sb("qx0 qx1 qx2 qx3", C, X4)
_sb("sx0 sx1 sx2 sx3", C, U8)
_sb("qa0 qa1 qa2 la0 la1 la2 qb0 qb1 qb2 qu qur qv", 128, X4)
_sb("sa0 sa1 sa2 ls0 ls1 ls2 sb0 sb1 sb2 su sur sv", 128, U8)
_sb("qw qe", 512, X4)
_sb("sw se", 512, U8)
_sb("W0 W1 W2", 352 + 16 * 52, F32)
_sb("IW", 768, F32)
_sb("S", 360, F32)
_sb("ysb cm C0 F Fw", C, F32)
_sb("nocc val val2 G Kv Pg P2", GW, F32)
_sb("lv", 8 * LV, F32)
_sb("vals", 576, F32)
_sb("mrep", 32, F32)
_sb("szi pi", 8, I32)
_sb("Lu", 8, U16)
_pool("pf", F32, ("PS ones z32 kz junk junk0 junk1", 96),
      ("mk rm nf ff fp xs Rp npc pcp Sn Ps zeros Ew E lane c0a c0b", 40),
      ("u16 uo16 uexp uo d16 dum yx ncd sel dd off", 56),
      ("eq zc z0 w16 Wb Y0 tt cI0 cI1 c20 c21 inv aa a2 oe cp mE0 mE1 ch cn sm b8", 24))
_pool("pj", I32, ("z1 di dj xi xj", 24))
_pool("pu", U16, ("Lup Lz Lr LmE Lm La Lc Lo Le Lx mu", 48), ("Lv0 Lv1", 64))

SEMAPHORES = ["V", "A", "P", "G", "sent", "arr0", "arr1", "arr2", "dsz", "dxa", "dxb", "du", "dv", "dw", "dws", "o1", "o2"]
PLANS = {}


def plan(ops):
    n = len(ops)
    key = tuple((o["q"], o["time"], tuple(sorted(o["need"]))) for o in ops)
    if key in PLANS:
        return PLANS[key][1]
    qn = [o["q"] for o in ops]

    def case(wake, gat, sca, trip):
        tm = [a + (x * gat + y * sca) * CY for a, x, y in (o["time"] for o in ops)]
        late = [o["late"] if o["late"] >= 0 else trip - 2000.0 * (o["late"] + 1.0) for o in ops]
        pre = [[(i, late[i] + wake) for i in o["need"]] + [(i, late[i] if o["ext"] else 0.0) for i in o["order"]] for o in ops]
        return tm, late, pre

    cases = [case(*c) for c in CASES]
    tm, late, pre = cases[0]
    suc = [[] for _ in ops]
    for j in range(n):
        for i, l in pre[j]:
            suc[i].append((j, l))

    def place(order, before, first):
        st = [0.0] * n
        busy = {q: [] for q in set(qn)}
        for j in order:
            r = first[j]
            for i, l in before[j]:
                if st[i] + tm[i] + l > r:
                    r = st[i] + tm[i] + l
            b = busy[qn[j]]
            k = len(b)
            while k and b[k - 1][1] > r:
                k -= 1
            while k < len(b) and b[k][0] < r + tm[j] - 1e-6:
                r = max(r, b[k][1])
                k += 1
            b.insert(k, (r, r + tm[j]))
            st[j] = r
        return st

    def length(order):
        total = 0.0
        for t2, l2, p2 in cases:
            end = [0.0] * n
            free = {}
            for j in order:
                r = free.get(qn[j], 0.0)
                for i, l in p2[j]:
                    if end[i] + l > r:
                        r = end[i] + l
                end[j] = free[qn[j]] = r + t2[j]
            total += max(end[j] + l2[j] for j in range(n))
        return total / len(cases)

    zero = [0.0] * n
    best, seed, order = None, 12345, list(range(n))
    for _ in range(TRIES):
        for _ in range(2):
            st = place(order, pre, zero)
            back = place(sorted(range(n), key=lambda j: (-st[j] - tm[j], -j)), suc, late)
            order = sorted(range(n), key=lambda j: (-back[j] - tm[j], j))
        st = place(order, pre, zero)
        order = sorted(range(n), key=lambda j: (st[j], j))
        m = length(order)
        if best is None or m < best[0]:
            best = (m, order, st)
        pos = []
        for j in range(n):
            seed = (seed * 1103515245 + 12345) % 2147483648
            x = best[2][j] + (seed / 2147483648.0 - 0.5) * 500.0
            pos.append(max([x] + [pos[i] + 1e-3 for i, l in pre[j]]))
        order = sorted(range(n), key=lambda j: (pos[j], j))
    PLANS[key] = best
    return best[1]


def rank_program(g, core, T, topo):
    rank = T.rank_of(core)
    if rank is None:
        return
    Op = AluOpType
    AF = ActivationFunctionType
    Q = {"V": g.vector, "A": g.scalar, "P": g.tensor, "G": g, "S": g.sync}
    ops = []
    hist = {}

    def v(name, a=0, b=None, s=1):
        if name in POOL:
            buf, o, n = POOL[name]
            return (buf, o + a, o + (n if b is None else b), s)
        if b is None:
            b = T[name].shape[1]
        return (name, a, b, s)

    def cols(x):
        m = 0
        if x[0] == "ps":
            for c in (x[1], x[2] - (1 if x[3] > 0 else -1)):
                m |= 1 << (c // 512)
            return m
        if x[3] == 1:
            return ((1 << (x[2] - x[1])) - 1) << x[1]
        for c in range(x[1], x[2], x[3]):
            m |= 1 << c
        return m

    def ap(x):
        if isinstance(x, (int, float)) or x is None:
            return x
        if len(x) == 2:
            return ap(x[0]).indirect(ap(x[1]))
        if x[3] == 1:
            return T[x[0]][:, x[1]:x[2]]
        return T[x[0]][:, x[1]:(x[2] if x[2] >= 0 else None):x[3]]

    def width(x):
        return 16 * (x[1][2] - x[1][1]) if len(x) == 2 else len(range(x[1], x[2], x[3]))

    def cost(o, a, k=1.0):
        if len(o) == 2:
            return (50.0, 0, width(a))
        if len(a) == 2:
            return (50.0, width(a), 0)
        return (max(64, width(a) * k) * CY, 0, 0)

    def issue(q, make, reads, writes, time, sem=None, inc=1, late=0.0, deps=(), ext=None):
        acc = []
        for x in reads:
            if isinstance(x, (int, float)) or x is None:
                continue
            for y in (x if len(x) == 2 else (x,)):
                acc.append((y[0], cols(y), y[0] == "ps"))
        for x in writes:
            if len(x) == 2:
                acc.append((x[1][0], cols(x[1]), False))
                x = x[0]
            acc.append((x[0], cols(x), True))
        need = set()
        for name, m, wr in acc:
            for hm, hw, j in hist.get(name, []):
                if hm & m and (hw or wr):
                    need.add(j)
        me = len(ops)
        ops.append({"q": q, "make": make, "need": need, "time": time if isinstance(time, tuple) else (time, 0, 0),
                    "sem": sem or q, "inc": inc, "late": late, "order": set(deps), "ext": ext})
        for name, m, wr in acc:
            h = hist.setdefault(name, [])
            if wr:
                h[:] = [e for e in h if e[0] & ~m]
            h.append((m, wr, me))
        return me

    V = g.vector

    def tt(o, a, b, op):
        k = 1.0 if "ps" in (a[0], b[0]) else 2.0
        issue("V", lambda: V.tensor_tensor(ap(o), ap(a), ap(b), op), [a, b], [o], cost(o, a, k))

    def ts(o, a, s1, op0, s2=None, op1=None):
        if op1 is None:
            issue("V", lambda: V.tensor_scalar(ap(o), ap(a), ap(s1), None, op0), [a, s1], [o], cost(o, a))
        else:
            issue("V", lambda: V.tensor_scalar(ap(o), ap(a), ap(s1), ap(s2), op0, op1), [a, s1, s2], [o], cost(o, a))

    def cp(o, a):
        issue("V", lambda: V.tensor_copy(ap(o), ap(a)), [a], [o], cost(o, a))

    def scan(o, d0, d1, init, op0, op1):
        issue("V", lambda: V.tensor_tensor_scan(ap(o), ap(d0), ap(d1), ap(init), op0, op1), [d0, d1, init], [o], cost(o, d0))

    def ms(o, c):
        issue("V", lambda: V.memset(ap(o), c), [], [o], cost(o, o, 0.5))

    def act(o, a, scale=1.0, bias=None, acc=None, relu=False):
        if acc is not None:
            issue("A", lambda: g.scalar.activation(ap(o), ap(a), AF.Identity, bias=bias, accum_out=ap(acc)), [a], [o, acc],
                  cost(o, a)[0] + 20)
        elif bias is None and not relu:
            issue("A", lambda: g.scalar.activation(ap(o), ap(a), AF.Copy, scale=scale), [a], [o], cost(o, a))
        else:
            fn = AF.Relu if relu else AF.Identity
            issue("A", lambda: g.scalar.activation(ap(o), ap(a), fn, bias=ap(bias or 0.0), scale=scale), [a, bias], [o], cost(o, a))

    def iota(o, pat, base=0, cm=0):
        issue("G", lambda: g.iota(ap(o), pat, base, cm, allow_small_or_imprecise_dtypes=True), [], [o], 130 + 2 * CY * width(o))

    def quant(q, s, a):
        issue("V", lambda: V.quantize_mx(ap(q), ap(s), ap(a)), [a], [q, s], 15 + 0.275 * width(a))

    def mm(bank, n, wq, ws, xq, xs, deps=(), ext=None):
        o = v("ps", 512 * bank, 512 * bank + n)
        issue("P", lambda: g.tensor.matmul_mx(ap(o), ap(wq), ap(ws), ap(xq), ap(xs), True, True), [wq, ws, xq, xs], [o],
              (n + 16) * 1.25, deps=deps, ext=ext)

    def dma(q, out, in_, reads, writes, sem, late, deps=()):
        return issue(q, lambda: Q[q].dma_start(out, in_), reads, writes, 80.0, sem, 16, late, deps)

    flip = [(rank >> t) & 1 for t in range(R)]
    c1 = CUT[1]

    d = dma("S", T.szi[:, 0:2], T.sz[:], [], [v("szi", 0, 2)], "dsz", 2000.0)
    e = dma("A", T.ut[:], T.u[:], [], [v("ut")], "du", 2500.0)
    d = dma("S", T.X0[:, 128:128 + 4 * c1], T.x[:, 0:4 * c1], [], [v("X0", 128, 128 + 4 * c1)], "dxa", 3200.0, [d])
    e = dma("A", T.X0[:, 128 + 4 * c1:XW], T.x[:, 4 * c1:4 * C], [], [v("X0", 128 + 4 * c1, XW)], "dxb", 3500.0, [e])
    d = dma("S", T.qw[:].bitcast(dt.uint8), T.wc[:], [v("X0", 128, XW)], [v("qw")], "dw", 3500.0, [d])
    d = dma("S", T.sw[:], T.ws[:], [], [v("sw")], "dws", 3500.0, [d])
    d = dma("S", T.vt[:], T.v[:], [], [v("vt")], "dv", 4000.0, [d])

    issue("G", lambda: g.iota(T.pi[:, 0:1], [[0, 1]], 0, 1), [], [v("pi", 0, 1)], 135.0)
    iota(v("lane", 0, 32), [[0, 2], [1, 16]])
    iota(v("IW", 0, 360), [[1, 360]], -1)
    iota(v("IW", 360, 768), [[1, 408]], 359)
    iota(v("z32"), [[32, 12], [0, 8]])
    iota(v("kz"), [[32 - 8192, 12], [-1024, 8]], 98304)
    iota(v("d16", 0, 50), [[16, 50]], C)
    iota(v("u16", 0, 48), [[16, 3], [0, 16]])
    iota(v("uo16", 0, 48), [[128, 3], [-O0, 2], [-1, 8]], O0 + 7)
    iota(v("zc", 0, 16), [[16, 2], [0, 8]], -18)
    iota(v("cm"), [[0, C]], -1023)
    for t in range(R):
        iota(v("W%d" % t, 0, C), [[0, C]], -8000000)
    for f in sorted(set(flip)):
        s = -1 if f else 1
        iota(v("cI%d" % f, 0, 16), [[-1, 2], [s, 4], [0, 2]], 4 if f else 1)
        iota(v("c2%d" % f, 0, 8), [[1024 * s, 4], [0, 2]], PAD + 1024 * (100 if f else 97))
    for j, c in enumerate((15, 7, 1, 8)):
        ts(v("pi", 4 + j, 5 + j), v("pi", 0, 1), c, Op.bitwise_and)
    cp(v("cp", 0, 4), v("pi", 4, 8))
    r_ = v("cp", 0, 1)
    ms(v("zeros"), 0.0)
    ms(v("ones"), 1.0)
    for t in range(R):
        ms(v("X%d" % t, 0, 128), 0.0)
    ms(v("E", 0, 1), 0.0)
    ms(v("S", C, 360), -1e29)
    ms(v("mk", 0, 1), 0.0)
    ms(v("Wb", 0, 1), 0.0)
    ms(v("PS", 32, 64), 0.0)
    ms(v("Rp", 0, 32), 9e29)
    ms(v("Rp", 0, 32, 4), -2e29)
    act(v("cp", 4, 5), r_, 1.0, 1.0)
    ts(v("cp", 14, 15), r_, 15.0, Op.is_lt, -BIG, Op.mult)
    act(v("cp", 5, 6), v("cp", 14, 15), 1.0, -1.0)
    act(v("cp", 6, 7), r_, 1.0, -32.0)
    act(v("cp", 7, 8), r_, 1.0, -16.0)
    base = 480.0 - 1.0 + PAD
    act(v("cp", 8, 9), r_, 1.0, base)
    act(v("cp", 9, 10), r_, 1.0, base + 16.0)
    act(v("cp", 10, 11), r_, -1.0, 32.0)
    act(v("cp", 11, 12), r_, -1.0, 16.0)
    act(v("cp", 12, 13), r_, 8.0)
    act(v("cp", 13, 14), v("cp", 1, 2), -4.0, 31.0)
    ts(v("c0a", 0, 32), v("lane", 0, 32), r_, Op.is_equal, -1e9, Op.mult)
    ts(v("c0b", 0, 32), v("lane", 0, 32), v("cp", 4, 5), Op.is_equal, BIG, Op.mult)
    tt(v("C0", 0, 32), v("c0a", 0, 32), v("c0b", 0, 32), Op.add)
    for a, n in ((32, 32), (64, 64), (128, 128), (256, 96)):
        act(v("C0", a, a + n), v("C0", 0, n))
    ts(v("LmE", 0, 1), v("cp", 3, 4), 0.25, Op.mult, v("cp", 2, 3), Op.add)
    ts(v("Lu", 0, 8), v("lane", 0, 8), 16.0, Op.mult)
    ts(v("Lup", 0, 6), v("zeros", 0, 6), v("cp", 13, 14), Op.add)
    ts(v("Lup", 6, 7), v("cp", 1, 2), -4.0, Op.mult, 95.0, Op.add)
    ts(v("Lz", 0, 1), v("cp", 1, 2), 4.0, Op.mult, 67.0, Op.add)
    ts(v("Lr", 0, 3), v("zeros", 0, 3), r_, Op.add)
    act(v("npc", 0, 32), v("IW", 1, 33), 1.0, -32.0)
    act(v("pcp", 0, 32), v("IW", 1, 33), -1.0, 32.0)
    for h in (0, 1):
        o = O0 * (1 - h)
        act(v("Pg", o, o + 96), v("z32"), -1.0, v("cp", 10 + h, 11 + h))
        act(v("Kv", o, o + 96), v("kz"), 1.0, v("cp", 8 + h, 9 + h))
        act(v("P2", o, o + 96), v("z32"), 1.0, v("cp", 8 + h, 9 + h))
        ts(v("Pg", O0 + 96 + 8 * h, O0 + 104 + 8 * h), v("zeros", 0, 8), r_, Op.add, 16.0 * h - 33.0, Op.add)
    for nm, c in (("Kv", 0.0), ("P2", base), ("nocc", 1.0), ("G", 0.0)):
        act(v(nm, 96, O0), v("IW", 0, O0 - 96), 0.0, c)
    act(v("dum", 0, 50), v("d16", 0, 50), 1.0, r_)
    act(v("uexp", 0, 48), v("u16", 0, 48), 1.0, r_)
    act(v("junk", 0, 48), v("u16", 0, 48), 0.0, v("cp", 12, 13))
    tt(v("uo16", 0, 48), v("uo16", 0, 48), v("junk", 0, 48), Op.add)
    act(v("uo", 0, 48), v("uo16", 0, 48), 0.125)
    act(v("onb"), v("IW", 0, 512), 0.0, 1.0)
    for b in range(4):
        o = v("Et", 512 * b, 512 * (b + 1))
        issue("G", lambda o=o, b=b: g.affine_select(ap(o), T.onb[:], [[-1, 128], [256, 4]], Op.is_equal, 0.0, -256 * b, 1),
              [v("onb")], [o], 170 + 1024 * CY)
    quant(v("qe"), v("se"), v("Et"))
    quant(v("qv"), v("sv"), v("vt"))
    quant(v("qu"), v("su"), v("ut"))
    issue("V", lambda: V.tensor_copy(T.qur[:].bitcast(dt.uint32), T.qu[:].bitcast(dt.uint32).indirect(T.Lu[:, 0:8])),
          [v("qu"), v("Lu", 0, 8)], [v("qur")], 250.0)
    issue("A", lambda: g.scalar.activation(T.sur[:], T.su[:].indirect(T.Lu[:, 0:8]), AF.Copy), [v("su"), v("Lu", 0, 8)], [v("sur")], 250.0)

    def sizes(e, f, more):
        mE = "mE%d" % e
        act(v("mrep", 0, 32), (v("IW", 0, 360), v("mu", 0, 2)), 1.0, 1.0)
        scan(v("E", 1, 33), v("mrep", 0, 32), v("zeros", 0, 32), 0.0, Op.add, Op.add)
        scan(v("Ew", 0, 32), v("C0", 0, 32), v("E", 1, 33), 0.0, Op.add, Op.max)
        act(v(mE, 2, 4), v("Ew", 15, 32, 16), 1.0, v("cp", 5, 6))
        for h in (0, 1):
            act(v("sm", 4 + h, 5 + h), v(mE, h, h + 1), -1.0, v(mE, 2 + h, 3 + h))
        tt(v("tt", 0, 16), (v(mE, 0, 4), v("LmE", 0, 1)), v("cI%d" % f, 0, 16), Op.subtract)
        act(v("inv", 0, 8), v("tt", 0, 8), -Z, relu=True)
        tt(v("aa", 0, 8), v("inv", 0, 8), v("tt", 8, 16), Op.add)
        if more:
            i0 = 6 if f else 0
            ts(v("Lm", 0, 2), v("aa", i0, i0 + 2), float(C), Op.min)
            tt(v("a2", 0, 8), v("aa", 0, 8), v("c2%d" % f, 0, 8), Op.add)
            ts(v("Lv%d" % e, 0, 2), v("sm", 4, 6), PAD + 1.0, Op.add)
            act(v("Sn", 0, 32), v("E", 0, 32), 1.0, -512.0)
            tt(v("xs", 0, 32), v("pcp", 0, 32), v("mrep", 0, 32), Op.subtract)

    cp(v("mu", 0, 2), v("szi", 0, 2))
    cp(v("mE0", 0, 2), v("szi", 0, 2))
    sizes(0, flip[0], True)

    def quant_mm(t, wq, ws):
        for h in (0, 1):
            a, b = CUT[h], CUT[h + 1]
            quant(v("qx%d" % t, a, b), v("sx%d" % t, a, b), v("X%d" % t, 128 + 4 * a, 128 + 4 * b))
            mm(h, b - a, wq, ws, v("qx%d" % t, a, b), v("sx%d" % t, a, b))

    for t in range(R):
        f, e, e2 = flip[t], t % 2, (t + 1) % 2
        fprev = flip[t - 1] if t else f
        X, Wn, A, B = "X%d" % t, "Wn%d" % t, "A%d" % t, "B%d" % t
        plane = lambda b, n: v(Wn, PL * b, PL * b + n)
        cell = lambda nm, h, n=96: v(nm, O0 * (1 - h), O0 * (1 - h) + n)
        quant_mm(t, v("qur"), v("sur"))
        act(v("S", 0, c1), v("ps", 0, c1))
        cp(v("S", c1, C), v("ps", 512, 512 + C - c1))
        for b in range(4):
            act(plane(b, HB), v(X, b, XW, 4), 64.0)
        cp(v("mk", 1, 33), (v("S"), v("Lm", 0, 2)))
        scan(v("rm", 0, 32), v("mk", 0, 32), v("Rp", 0, 32), 0.0, Op.max, Op.min)
        tt(v("ff", 0, 32), v("mk", 1, 33), v("rm", 0, 32), Op.is_gt)
        tt(v("nf", 0, 32), v("mk", 1, 33), v("rm", 0, 32), Op.is_le)
        tt(v("fp", 0, 32), v("ff", 0, 32), v("xs", 0, 32), Op.mult)
        scan(v("PS", 64, 96), v("nf", 0, 32), v("npc", 0, 32), 0.0, Op.mult, Op.min)
        scan(v("Ps", 0, 32), v("nf", 0, 32), v("Sn", 0, 32), 0.0, Op.mult, Op.min)
        scan(v("PS", 0, 32), v("nf", 0, 32), v("fp", 0, 32), 0.0, Op.mult, Op.add)
        tt(v("b8", 0, 8), v("Ps", 3, 32, 4), v("PS", 67, 96, 4), Op.subtract)
        PSw = v("PS", 0, 96)
        for j in range(8):
            act(v("val", j, O0 + 96, 8), v("Kv", j, O0 + 96, 8), 1.0, v("b8", 7 - j, 8 - j))
        for h in (0, 1):
            ts(v("eq", 8 * h, 8 * h + 8), v("PS", 67, 96, 4), v("cp", 6 + h, 7 + h), Op.is_equal, Z, Op.mult)
            act(v("junk", 8 * h, 8 * h + 8), v("eq", 8 * h, 8 * h + 8), bias=0.0, acc=v("ch", h, h + 1))
        tt(cell("nocc", 0, 112), (PSw, v("Lup", 0, 7)), cell("Pg", 0, 112), Op.is_gt)
        tt(cell("nocc", 1), (PSw, v("Lup", 0, 6)), cell("Pg", 1), Op.is_gt)
        for h in (0, 1):
            tt(cell("nocc", h, 8), cell("nocc", h, 8), v("nocc", O0 + 96 + 8 * h, O0 + 104 + 8 * h), Op.max)
            src = v("a2", h, 8, 2) if fprev == f else v("a2", 6 + h, -1, -2)
            ts(v("lv", LV * h, 8 * LV, 2 * LV), src, Z, Op.min, v("ch", h, h + 1), Op.max)
        for i in range(4):
            for h in (0, 1):
                k = LV * (2 * (3 - i if f else i) + h)
                j = LV * (2 * (4 - i if f else i - 1) + h)
                scan(v("lv", k + 1, k + 97), cell("nocc", h), cell("val", h) if i == 0 else v("lv", j, j + 96), v("lv", k, k + 1),
                     Op.mult, Op.max)
        cp(v("di", 0, 8), v("lv", 96, 8 * LV, LV))
        ts(v("dj", 0, 8), v("di", 0, 8), 1023, Op.bitwise_and)
        cp(v("La", 0, 8), v("dj", 0, 8))
        for b in range(4):
            if b < AV:
                ts(v(A, b, 512, 4), (plane(b, HB), v("La", 0, 8)), 0.015625, Op.mult)
            else:
                act(v(A, b, 512, 4), (plane(b, HB), v("La", 0, 8)), 0.015625)
        quant(v("qa%d" % t), v("sa%d" % t), v(A))
        peer = T.cores[rank ^ (1 << t)]
        rid, pid = topo.addr(peer, core)
        mask = topo.mask(core, peer)
        ne = len(topo.engines(core, peer))
        arr = "arr%d" % t

        def put(dst, src, arr=arr, pid=pid, rid=rid, mask=mask):
            g.remote_dma(dst, src, T.sem[arr], T.sem.sent, pid, rid, mask)

        s0 = issue("G", lambda t=t, put=put: put(T["la%d" % t][:].bitcast(dt.uint8), T["qa%d" % t][:].bitcast(dt.uint8)),
                   [v("qa%d" % t)], [], 300.0, "sent", ne, -1.0 - (t == 0))
        s1 = issue("G", lambda t=t, put=put: put(T["ls%d" % t][:], T["sa%d" % t][:]), [v("sa%d" % t)], [], 300.0, "sent", ne,
                   -1.0 - (t == 0), [s0])
        act(v("A64"), v(A), 64.0)

        mE, mN = "mE%d" % e, "mE%d" % e2
        for h in (0, 1):
            act(v("junk%d" % h), cell("nocc", h), bias=-1.0, acc=v("cn", h, h + 1))
            act(v("sm", 2 + h, 3 + h), v("ch", h, h + 1), -1.0, v(mE, h, h + 1), relu=True)
            act(v(mN, h, h + 1), v("cn", h, h + 1), -1.0, v("sm", 2 + h, 3 + h))
            act(v("sm", 10 + h, 11 + h), v("sm", 2 + h, 3 + h), -1024.0, v("dum", h, h + 1), relu=True)
        cp(v("mu", 0, 2), v(mN, 0, 2))
        sizes(e2, f, t < R - 1)
        for h in (0, 1):
            act(v("sm", 8 + h, 9 + h), v("cn", h, h + 1), 1.0, v(mN, 2 + h, 3 + h))
            scan(cell("G", h), v("ones"), cell("nocc", h), v("sm", 8 + h, 9 + h), Op.add, Op.subtract)
            ts(v("off", h, h + 1), v("sm", 4 + h, 5 + h), 1.0, Op.add, v("sm", 10 + h, 11 + h), Op.max)
        tt(v("oe", 0, 8), v("aa", 0, 8), v("dum", 0, 8), Op.min)
        cp(v("Le", 0, 8), v("oe", 0, 8))
        for j in range(8):
            act(v("val2", j, O0 + 96, 8), v("P2", j, O0 + 96, 8), 1.0, v("b8", 7 - j, 8 - j))
        for h in (0, 1):
            ts(v("z1", 8 * h, 8 * h + 8), v("PS", 3, 32, 4), 48.5 - 16 * h, Op.subtract, -0.03125, Op.mult)
        tt(v("z0", 0, 16), (PSw, v("Lz", 0, 1)), v("zc", 0, 16), Op.is_gt)
        tt(v("w16", 0, 16), v("z1", 0, 16), v("z0", 0, 16), Op.subtract)
        scan(v("Wb", 1, 17), v("w16", 0, 16), v("zeros", 0, 16), 0.0, Op.add, Op.add)
        tt(v("Y0", 0, 16), v("z1", 0, 16), v("Wb", 1, 17), Op.subtract)
        tt(v("ncd", 0, 48), (v("Wb", 0, 17), v("Lr", 0, 3)), v("uexp", 0, 48), Op.is_gt)
        tt(v("yx", 0, 48), (v("Y0", 0, 16), v("Lr", 0, 3)), v("uo", 0, 48), Op.add)
        scan(v("sel", 0, 48), v("ncd", 0, 48), v("yx", 0, 48), 0.0, Op.mult, Op.max)
        ts(v("Lc", 0, 3), v("sel", 15, 48, 16), 8.0, Op.mult)
        cp(v("Lv%d" % e, 2, 50), (v("val2", 0, O0 + 96), v("Lc", 0, 3)))
        act(v("vals"), (v("IW"), v("Lv%d" % e, 0, K + 2)))
        tt(v("dd", 0, 48), (v("nocc", 0, O0 + 96), v("Lc", 0, 3)), v("dum", 2, 50), Op.mult)
        tt(v("off", 2, 50), (v("G", 0, O0 + 96), v("Lc", 0, 3)), v("dd", 0, 48), Op.max)
        cp(v("Lo", 0, K + 2), v("off", 0, K + 2))
        W = "W%d" % t
        cp((v(W), v("Lo", 0, K + 2)), v("vals"))
        cp((v(W), v("Le", 0, 8)), v("IW", HB, HB + 128))
        scan(v("F"), v(W, 0, C), v("cm"), -2000.0, Op.max, Op.add)
        scan(v("Fw"), v("C0"), v("F"), 0.0, Op.add, Op.max)
        ts(v("xi", 0, 22), v("Fw", 15, C, 16), 2 * BIG, Op.add)
        ts(v("xj", 0, 22), v("xi", 0, 22), 1023, Op.bitwise_and)
        cp(v("Lx", 0, 22), v("xj", 0, 22))
        for b in range(4):
            mm(2 + b, 128, v("qe", 128 * b, 128 * b + 128), v("se", 128 * b, 128 * b + 128), v("la%d" % t), v("ls%d" % t),
               [s0, s1], (arr, 2 * ne))
            tt(v(B, b, 512, 4), v("ps", 512 * (2 + b) + 127, 512 * (2 + b) - 1, -1), v(A, b, 512, 4), Op.add)
        quant(v("qb%d" % t), v("sb%d" % t), v(B))
        Xn = "X%d" % (t + 1)
        for b in (2, 3, 0, 1):
            k = 6 + (b % 2) if b >= 2 else b
            mm(k, 128, v("qw", 128 * b, 128 * b + 128), v("sw", 128 * b, 128 * b + 128), v("qb%d" % t), v("sb%d" % t))
            tt(v(Wn, PL * b + HB, PL * b + PL), v("ps", 512 * k, 512 * k + 128), v("A64", b, 512, 4), Op.add)
            for h in (0, 1):
                o = v(Xn, 128 + 4 * CUT[h] + b, 128 + 4 * CUT[h + 1], 4)
                src = (plane(b, PL), v("Lx", CUT[h] // 16, CUT[h + 1] // 16))
                if (b, h) in XV:
                    ts(o, src, 0.015625, Op.mult)
                else:
                    act(o, src, 0.015625)

    dma("S", T.oz[:], T.mrep[0:128:16, 0:32], [v("mrep", 0, 32)], [], "o1", 2000.0)
    quant_mm(R, v("qv"), v("sv"))
    for h in (0, 1):
        a, b = CUT[h], CUT[h + 1]
        dma("S", T.oc[:, 4 * a:4 * b], T.qx3[:, a:b].bitcast(dt.uint8), [v("qx3", a, b)], [], "o1", 2500.0)
    act(v("ysb", 0, c1), v("ps", 0, c1))
    cp(v("ysb", c1, C), v("ps", 512, 512 + C - c1))
    dma("A", T.y[:, 0:c1], T.ysb[:, 0:c1], [v("ysb", 0, c1)], [], "o2", 2500.0)
    dma("A", T.y[:, c1:C], T.ysb[:, c1:C], [v("ysb", c1, C)], [], "o2", 2500.0)
    for k in range(4):
        dma("S", T.osc[4 * k:4 * k + 4, :], T.sx3[32 * k:32 * k + 4, :], [v("sx3")], [], "o1", 2000.0)

    know = {q: {} for q in Q}
    count = {}
    after = {}

    def wait(q, sem, c):
        if know[q].get(sem, 0) >= c:
            return
        Q[q].wait_ge(T.sem[sem], c)
        know[q][sem] = c
        for s, k in after.get((sem, c), {}).items():
            if know[q].get(s, 0) < k:
                know[q][s] = k

    for j in plan(ops):
        o = ops[j]
        need = {}
        for i in o["need"]:
            s, c = ops[i]["sem"], ops[i]["count"]
            need[s] = max(need.get(s, 0), c)
        if o["ext"]:
            wait(o["q"], *o["ext"])
        for s in sorted(need, key=lambda s: s == o["q"]):
            wait(o["q"], s, need[s])
        ins = o["make"]()
        s = o["sem"]
        count[s] = count.get(s, 0) + o["inc"]
        o["count"] = count[s]
        if ins is not None:
            ins.then_inc(T.sem[s], o["inc"])
        after[(s, count[s])] = dict(know[o["q"]])
    for s in sorted(count):
        wait("G" if s in ("sent", "G") else "S", s, count[s])
